import numpy as np
import ml_dtypes


def mxq(x, axis, fmt="e4m3"):
    dtype, down = {"e4m3": (ml_dtypes.float8_e4m3fn, 7), "e5m2": (ml_dtypes.float8_e5m2, 14)}[fmt]
    v = np.moveaxis(np.asarray(x, np.float32).astype(ml_dtypes.bfloat16).astype(np.float64), axis, -1)
    blocks = v.reshape(v.shape[:-1] + (-1, 32))
    amax = np.abs(blocks).max(-1, keepdims=True)
    byte = np.maximum(np.where(amax > 0, np.frexp(amax)[1] - 1 + 127, 0) - down, 1)
    scale = np.exp2(byte - 127.0)
    codes = (blocks / scale).astype(np.float32).astype(dtype).astype(np.float64)
    return np.moveaxis((codes * scale).reshape(v.shape), -1, axis)


WIDE = False


def mx_kscale(k):
    if not WIDE:
        return np.ones(k)
    levels = np.array([10, -10, 5, -5, 0])
    if k % 512:
        return np.exp2(np.random.permutation(np.resize(levels, k // 32))).repeat(32)
    a = np.empty((k // 512, 16))
    for p in range(k // 512):
        a[p, :8] = np.random.permutation(np.resize(levels, 8))
        for g in range(8):
            far = levels[np.abs(levels - a[p, g]) >= 10]
            a[p, g + 8] = far[np.random.randint(len(far))]
    return np.exp2(a.ravel()).repeat(32)


def f64(x):
    return np.asarray(x).astype(np.float64)


def striped(idx):
    return np.tile(idx.reshape(-1, 16).T, (8, 1)).astype(np.uint16)


def unstriped(offs):
    return offs[:16].T.reshape(-1).astype(np.int64)


def striped8(idx):
    return np.concatenate([x.reshape(-1, 16).T for x in idx]).astype(np.uint16)


def runs(offs, k):
    lists = np.stack([offs[16 * r : 16 * r + 16].T.reshape(-1) for r in range(8)]).astype(np.int64)
    return lists[np.arange(k) % 512 // 64]


def pack_weight(w):
    k, n = w.shape
    w = f64(np.asarray(w, np.float32).astype(ml_dtypes.bfloat16)).reshape(k // 32, 32, n)
    amax = np.abs(w).max(1)
    byte = np.clip(np.where(amax > 0, np.frexp(amax)[1] - 1 + 127 - 7, 1), 1, 254)
    scaled = (w * np.exp2(127.0 - byte)[:, None, :]).reshape(k, n).astype(np.float32)
    words = np.ascontiguousarray(scaled.reshape(k // 512, 128, 4, n).transpose(0, 1, 3, 2)).astype(ml_dtypes.float8_e4m3fn).view(np.uint8)
    return words, np.ascontiguousarray(byte.astype(np.uint8).reshape(k // 512, 16, n))


def unpack_weight(words, scales):
    g, p, n, _ = words.shape
    vals = np.ascontiguousarray(words).view(ml_dtypes.float8_e4m3fn).astype(np.float64) * np.repeat(np.exp2(scales.astype(np.float64) - 127.0), 8, axis=1)[..., None]
    return vals.transpose(0, 1, 3, 2).reshape(g * 512, n)


def relu(v):
    return np.maximum(v, 0.0)


def sigmoid(v):
    return 1.0 / (1.0 + np.exp(-np.maximum(v, -700.0)))


K, T, S, N, H = 512, 2048, 256, 512, 512


def setup_inputs():
    n = np.random.standard_normal
    s = mx_kscale(K)[:, None]
    u = mx_kscale(H)
    packed_xT = pack_weight(n((K, T)) * s)
    return {
        "x_words": packed_xT[0],
        "x_scales": packed_xT[1],
        "w1": (n((K, H)) / np.sqrt(K) / s).astype(np.float32),
        "w2": (n((K, H)) / np.sqrt(K) / s).astype(np.float32),
        "sl": np.random.uniform(1.0, 2.0, (H, 1)).astype(np.float32),
        "th": (0.5 * n((H, 1))).astype(np.float32),
        "sl2": np.random.uniform(1.0, 2.0, (H, 1)).astype(np.float32),
        "th2": (0.5 * n((H, 1))).astype(np.float32),
        "gn": (np.random.uniform(0.5, 1.5, (H, 1)) * u[:, None]).astype(np.float32),
        "w3": (n((H, N)) / np.sqrt(H) / u[:, None]).astype(np.float32),
        "offs": striped(np.random.permutation(T)[:S]),
        "two": striped(np.random.permutation(T)[:S]),
        "n1": striped(np.random.permutation(S)),
        "n2": striped(np.random.permutation(S)),
        "n3": striped8(np.stack([np.random.permutation(S) for _ in range(8)])),
        "n4": striped8(np.stack([np.random.permutation(S) for _ in range(8)])),
    }


def reference(x_words, x_scales, w1, w2, sl, th, sl2, th2, gn, w3, offs, two, n1, n2, n3, n4):
    xq = unpack_weight(x_words, x_scales)[:, unstriped(offs)]
    y = mxq(f64(w1), 0, "e4m3").T @ xq
    sg = sigmoid(f64(sl) * (y[:, unstriped(n1)] - f64(th)))
    x_two = unpack_weight(x_words, x_scales)[:, unstriped(two)]
    d = mxq(f64(w2), 0, "e4m3").T @ x_two
    sg2 = sigmoid(f64(sl2) * (d[:, unstriped(n2)] - f64(th2)))
    z = f64(gn) * (sg * d + sg2 * y)
    h = mxq(f64(w3), 0, "e4m3").T @ mxq(z, 0, "e4m3")
    return relu(h - (h[np.arange(N)[:, None], runs(n3, N)])) + 0.5 * (relu(h[np.arange(N)[:, None], runs(n4, N)] - h))

@@ -1,0 +1,226 @@
+from contextlib import ExitStack
+
+import concourse.mybir as mybir
+
+K, T, S, H, N = 512, 2048, 256, 512, 512
+FLOPS = 2 * K * H * S * 2 + 2 * H * N * S
+
+F32 = mybir.dt.float32
+BF16 = mybir.dt.bfloat16
+I32 = mybir.dt.int32
+U32 = mybir.dt.uint32
+U16 = mybir.dt.uint16
+U8 = mybir.dt.uint8
+FP8X4 = mybir.dt.float8_e4m3fn_x4
+ALU = mybir.AluOpType
+ACT = mybir.ActivationFunctionType
+
+P = 128
+PACK = 4
+HALF = S // 2
+LIST_COLS = S // 16
+
+
+def tile_picked_twlcxbhinge_none_p_kernel(
+    tc, x_words, x_scales, w1, w2, sl, th, sl2, th2, gn, w3, offs, two, n1, n2, n3, n4, out
+):
+    nc = tc.nc
+    with ExitStack() as ctx:
+        sb = ctx.enter_context(tc.tile_pool(name="sb", bufs=1))
+        ps = ctx.enter_context(tc.psum_pool(name="ps", bufs=1))
+
+        def load_list(name, src):
+            tile = sb.tile([P, LIST_COLS], U16, name=name)
+            nc.sync.dma_start(tile[:], src)
+            return tile
+
+        def load_weight(name, src):
+            tile = sb.tile([P, PACK, H], F32, name=name)
+            nc.sync.dma_start(out=tile[:], in_=src.rearrange("(p j) c -> p j c", j=PACK))
+            return tile
+
+        def load_rows(name, src, queue=nc.sync):
+            tile = sb.tile([P, PACK], F32, name=name)
+            queue.dma_start(out=tile[:], in_=src.rearrange("(p t) o -> p (t o)", t=PACK))
+            return tile
+
+        def half_list(tile, half):
+            return tile[:, half * LIST_COLS // 2 : (half + 1) * LIST_COLS // 2]
+
+        def deal(copy, dealt, raw, m0, m1):
+            copy(
+                out=dealt[:].rearrange("p (t m j) -> p m j t", t=PACK, j=PACK)[:, m0:m1],
+                in_=raw[:].rearrange("p j (m t) -> p m j t", t=PACK)[:, m0:m1],
+            )
+
+        def quantize(name, values, width):
+            codes = sb.tile([P, width], U32, name=name + "_codes", align_bytes=64)
+            scales = sb.tile([P, width], U8, name=name + "_scales", align_bytes=64)
+            nc.vector.quantize_mx(out=codes[:].bitcast(FP8X4), scales=scales[:], in_=values)
+            return codes, scales
+
+        def product(acc, lhs, rhs):
+            nc.tensor.matmul_mx(
+                out=acc,
+                lhsT=lhs[0][:].bitcast(FP8X4),
+                lhsT_scale=lhs[1][:],
+                rhs=rhs[0][:].bitcast(FP8X4),
+                rhs_scale=rhs[1][:],
+                start=True,
+                stop=True,
+            )
+
+        x_bytes = sb.tile([P, T], U8, name="x_bytes", align_bytes=64)
+        nc.vector.memset(x_bytes[:].bitcast(I32), 0)
+        x_rows = sb.tile([P, T], U8, name="x_rows", align_bytes=64)
+        for q in range(4):
+            nc.scalar.dma_start(out=x_rows[32 * q : 32 * q + 4, :].bitcast(I32), in_=x_scales[0][4 * q : 4 * q + 4, :].bitcast(I32))
+        offs_sb = load_list("offs_sb", offs)
+        two_sb = load_list("two_sb", two)
+        w1_raw = load_weight("w1_raw", w1)
+        x_table = sb.tile([P, T], U32, name="x_table", align_bytes=64)
+        nc.sync.dma_start(out=x_table[:].bitcast(I32), in_=x_words[0].rearrange("p c r -> p (c r)").bitcast(I32))
+        n1_sb = load_list("n1_sb", n1)
+        sl_sb = load_rows("sl_sb", sl)
+        th_sb = load_rows("th_sb", th)
+        n2_sb = load_list("n2_sb", n2)
+        gn_sb = load_rows("gn_sb", gn)
+        w2_raw = load_weight("w2_raw", w2)
+        sl2_sb = load_rows("sl2_sb", sl2)
+        th2_sb = load_rows("th2_sb", th2)
+        w3_raw = load_weight("w3_raw", w3)
+        n3_sb = load_list("n3_sb", n3)
+        n4_sb = load_list("n4_sb", n4)
+
+        for q in range(4):
+            rows = slice(32 * q, 32 * q + 4)
+            nc.vector.tensor_copy(out=x_bytes[rows, :].bitcast(I32), in_=x_rows[rows, :].bitcast(I32))
+        picked_bytes = []
+        for name, picks in (("y", offs_sb), ("d", two_sb)):
+            got = sb.tile([P, S], U8, name=name + "_bytes", align_bytes=64)
+            nc.vector.tensor_copy(got[:], x_bytes[:].indirect(picks[:]))
+            picked_bytes.append(got)
+        bias1 = sb.tile([P, PACK], F32, name="bias1")
+        nc.vector.scalar_tensor_tensor(out=bias1[:], in0=sl_sb[:], scalar=-1.0, in1=th_sb[:], op0=ALU.mult, op1=ALU.mult)
+
+        w1_dealt = sb.tile([P, PACK * H], BF16, name="w1_dealt", align_bytes=64)
+        deal(nc.vector.tensor_copy, w1_dealt, w1_raw, 0, 64)
+        deal(nc.scalar.copy, w1_dealt, w1_raw, 64, P)
+        w1_q = [quantize(f"w1_{t}", w1_dealt[:, t * H : (t + 1) * H], P) for t in range(PACK)]
+        bias2 = sb.tile([P, PACK], F32, name="bias2")
+        nc.vector.scalar_tensor_tensor(out=bias2[:], in0=sl2_sb[:], scalar=-1.0, in1=th2_sb[:], op0=ALU.mult, op1=ALU.mult)
+
+        picked = []
+        for name, picks, got_bytes in (("y", offs_sb, picked_bytes[0]), ("d", two_sb, picked_bytes[1])):
+            got = sb.tile([P, S], U32, name=name + "_words", align_bytes=64)
+            nc.vector.tensor_copy(got[:], x_table[:].indirect(picks[:]))
+            picked.append((got, got_bytes))
+
+        y_ps, sg = [], []
+        for t in range(PACK):
+            acc = ps.tile([P, S], F32, name=f"y_ps{t}", tag=f"bank{t}")
+            product(acc[:], w1_q[t], picked[0])
+            y_ps.append(acc)
+        for t in range(PACK):
+            y_sb = sb.tile([P, S], F32, name=f"y_sb{t}")
+            nc.vector.tensor_copy(out=y_sb[:], in_=y_ps[t][:])
+            gate = sb.tile([P, S], F32, name=f"sg{t}")
+            for half in range(2):
+                nc.scalar.activation(
+                    out=gate[:, half * HALF : (half + 1) * HALF],
+                    in_=y_sb[:].indirect(half_list(n1_sb, half)),
+                    func=ACT.Sigmoid,
+                    bias=bias1[:, t : t + 1],
+                    scale=sl_sb[:, t : t + 1],
+                )
+            sg.append(gate)
+
+        w2_dealt = sb.tile([P, PACK * H], BF16, name="w2_dealt", align_bytes=64)
+        deal(nc.vector.tensor_copy, w2_dealt, w2_raw, 0, P)
+        d_ps, d_sb = [], []
+        for t in range(PACK):
+            w2_q = quantize(f"w2_{t}", w2_dealt[:, t * H : (t + 1) * H], P)
+            acc = ps.tile([P, S], F32, name=f"d_ps{t}", tag=f"bank{PACK + t}")
+            product(acc[:], w2_q, picked[1])
+            d_ps.append(acc)
+        for t in range(PACK):
+            window = sb.tile([P, S], F32, name=f"d_sb{t}")
+            nc.scalar.copy(out=window[:], in_=d_ps[t][:])
+            d_sb.append(window)
+        gated_d = sb.tile([P, PACK, S], F32, name="gated_d")
+        for t in range(PACK):
+            nc.vector.scalar_tensor_tensor(
+                out=gated_d[:, t, :], in0=sg[t][:], scalar=gn_sb[:, t : t + 1], in1=d_ps[t][:], op0=ALU.mult, op1=ALU.mult
+            )
+
+        w3_dealt = sb.tile([P, PACK * H], BF16, name="w3_dealt", align_bytes=64)
+        deal(nc.vector.tensor_copy, w3_dealt, w3_raw, 0, P)
+
+        w3_q = [quantize(f"w3_{t}", w3_dealt[:, t * H : (t + 1) * H], P) for t in range(PACK)]
+
+        sg2 = {}
+        for half in range(2):
+            for t in range(PACK):
+                gate = sb.tile([P, HALF], F32, name=f"sg2_{t}_{half}")
+                nc.scalar.activation(
+                    out=gate[:],
+                    in_=d_sb[t][:].indirect(half_list(n2_sb, half)),
+                    func=ACT.Sigmoid,
+                    bias=bias2[:, t : t + 1],
+                    scale=sl2_sb[:, t : t + 1],
+                )
+                sg2[t, half] = gate
+
+        z_q = []
+        for half in range(2):
+            cols = slice(half * HALF, (half + 1) * HALF)
+            gated_y = sb.tile([P, PACK, HALF], F32, name=f"gated_y{half}")
+            for t in range(PACK):
+                nc.vector.scalar_tensor_tensor(
+                    out=gated_y[:, t, :], in0=sg2[t, half][:], scalar=gn_sb[:, t : t + 1], in1=y_ps[t][:, cols],
+                    op0=ALU.mult, op1=ALU.mult,
+                )
+            z = sb.tile([P, PACK * HALF], BF16, name=f"z{half}", align_bytes=64)
+            nc.vector.tensor_tensor(
+                out=z[:].rearrange("p (c i t) -> p c t i", i=4, t=PACK),
+                in0=gated_d[:, :, cols].rearrange("p t (c i) -> p c t i", i=4),
+                in1=gated_y[:].rearrange("p t (c i) -> p c t i", i=4),
+                op=ALU.add,
+            )
+            z_q.append(quantize(f"z{half}", z[:], HALF))
+
+        h_sb = [sb.tile([P, S], F32, name=f"h_sb{t}") for t in range(PACK)]
+        for half in range(2):
+            for t in range(PACK):
+                acc = ps.tile([P, HALF], F32, name=f"h_ps{t}_{half}", tag=f"bank{PACK * (1 - half) + t}")
+                product(acc[:], w3_q[t], z_q[half])
+                nc.vector.tensor_copy(out=h_sb[t][:, half * HALF : (half + 1) * HALF], in_=acc[:])
+
+        out_rows = out.rearrange("(p t) j -> p t j", t=PACK)
+        for t in range(PACK):
+            at_n3 = sb.tile([P, S], F32, name=f"at_n3_{t}")
+            at_n4 = sb.tile([P, S], F32, name=f"at_n4_{t}")
+            for half in range(2):
+                nc.scalar.activation(
+                    out=at_n3[:, half * HALF : (half + 1) * HALF], in_=h_sb[t][:].indirect(half_list(n3_sb, half)), func=ACT.Copy
+                )
+            for half in range(2):
+                nc.scalar.activation(
+                    out=at_n4[:, half * HALF : (half + 1) * HALF], in_=h_sb[t][:].indirect(half_list(n4_sb, half)),
+                    func=ACT.Copy, scale=0.5,
+                )
+            above = sb.tile([P, S], F32, name=f"above{t}")
+            nc.vector.tensor_tensor(out=above[:], in0=h_sb[t][:], in1=at_n3[:], op=ALU.subtract)
+            hinge = sb.tile([P, S], F32, name=f"hinge{t}")
+            nc.vector.tensor_scalar(out=hinge[:], in0=above[:], scalar1=0.0, scalar2=None, op0=ALU.max)
+            below = sb.tile([P, S], F32, name=f"below{t}")
+            result = sb.tile([P, S], F32, name=f"result{t}")
+            pieces = [slice(0, HALF), slice(HALF, S)] if t == PACK - 1 else [slice(0, S)]
+            for cols in pieces:
+                nc.vector.scalar_tensor_tensor(
+                    out=below[:, cols], in0=h_sb[t][:, cols], scalar=-0.5, in1=at_n4[:, cols], op0=ALU.mult, op1=ALU.add
+                )
+                nc.vector.scalar_tensor_tensor(
+                    out=result[:, cols], in0=below[:, cols], scalar=0.0, in1=hinge[:, cols], op0=ALU.max, op1=ALU.add
+                )
+                nc.sync.dma_start(out=out_rows[:, t, cols], in_=result[:, cols])

@@ -35,192 +35,220 @@ def tile_picked_twlcxbhinge_none_p_kernel(
             return tile
 
         def load_weight(name, src):
-            tile = sb.tile([P, PACK, H], F32, name=name)
+            tile = sb.tile([P, PACK, src.shape[1]], F32, name=name)
             nc.sync.dma_start(out=tile[:], in_=src.rearrange("(p j) c -> p j c", j=PACK))
             return tile
 
-        def load_rows(name, src, queue=nc.sync):
+        def load_rows(name, src):
             tile = sb.tile([P, PACK], F32, name=name)
-            queue.dma_start(out=tile[:], in_=src.rearrange("(p t) o -> p (t o)", t=PACK))
+            nc.sync.dma_start(out=tile[:], in_=src.rearrange("(p t) o -> p (t o)", t=PACK))
             return tile
 
         def half_list(tile, half):
             return tile[:, half * LIST_COLS // 2 : (half + 1) * LIST_COLS // 2]
 
-        def deal(copy, dealt, raw, m0, m1):
+        def deal(copy, dealt, raw, m0, m1, first=0):
             copy(
                 out=dealt[:].rearrange("p (t m j) -> p m j t", t=PACK, j=PACK)[:, m0:m1],
-                in_=raw[:].rearrange("p j (m t) -> p m j t", t=PACK)[:, m0:m1],
+                in_=raw[:].rearrange("p j (m t) -> p m j t", t=PACK)[:, m0 - first : m1 - first],
             )
 
-        def quantize(name, values, width):
-            codes = sb.tile([P, width], U32, name=name + "_codes", align_bytes=64)
+        def quantize(name, values, width, tag=None):
+            codes = sb.tile([P, width], U32, name=name + "_codes", tag=tag or name + "_codes", align_bytes=64)
             scales = sb.tile([P, width], U8, name=name + "_scales", align_bytes=64)
             nc.vector.quantize_mx(out=codes[:].bitcast(FP8X4), scales=scales[:], in_=values)
-            return codes, scales
+            return codes[:], scales[:]
+
+        def columns(operand, t):
+            return operand[0][:, t * P : (t + 1) * P], operand[1][:, t * P : (t + 1) * P]
 
         def product(acc, lhs, rhs):
             nc.tensor.matmul_mx(
                 out=acc,
-                lhsT=lhs[0][:].bitcast(FP8X4),
-                lhsT_scale=lhs[1][:],
-                rhs=rhs[0][:].bitcast(FP8X4),
-                rhs_scale=rhs[1][:],
+                lhsT=lhs[0].bitcast(FP8X4),
+                lhsT_scale=lhs[1],
+                rhs=rhs[0].bitcast(FP8X4),
+                rhs_scale=rhs[1],
                 start=True,
                 stop=True,
             )
 
+        def gather(out_ap, window, picks, func, **kw):
+            nc.scalar.activation(out=out_ap, in_=window[:].indirect(picks), func=func, **kw)
+
+        def neg_product(name, a, b):
+            prod = sb.tile([P, PACK], F32, name=name + "_prod")
+            nc.gpsimd.tensor_tensor(out=prod[:], in0=a[:], in1=b[:], op=ALU.mult)
+            neg = sb.tile([P, PACK], F32, name=name)
+            nc.gpsimd.tensor_scalar(out=neg[:], in0=prod[:], scalar1=-1.0, scalar2=0.0, op0=ALU.mult, op1=ALU.add)
+            return neg
+
         x_bytes = sb.tile([P, T], U8, name="x_bytes", align_bytes=64)
         nc.vector.memset(x_bytes[:].bitcast(I32), 0)
-        x_rows = sb.tile([P, T], U8, name="x_rows", align_bytes=64)
+        w1_raw = load_weight("w1_raw", w1)
         for q in range(4):
-            nc.scalar.dma_start(out=x_rows[32 * q : 32 * q + 4, :].bitcast(I32), in_=x_scales[0][4 * q : 4 * q + 4, :].bitcast(I32))
+            nc.sync.dma_start(out=x_bytes[32 * q : 32 * q + 4, :].bitcast(I32), in_=x_scales[0][4 * q : 4 * q + 4, :].bitcast(I32))
         offs_sb = load_list("offs_sb", offs)
         two_sb = load_list("two_sb", two)
-        w1_raw = load_weight("w1_raw", w1)
         x_table = sb.tile([P, T], U32, name="x_table", align_bytes=64)
         nc.sync.dma_start(out=x_table[:].bitcast(I32), in_=x_words[0].rearrange("p c r -> p (c r)").bitcast(I32))
-        n1_sb = load_list("n1_sb", n1)
         sl_sb = load_rows("sl_sb", sl)
         th_sb = load_rows("th_sb", th)
+        n1_sb = load_list("n1_sb", n1)
+        w2_raw = [load_weight(f"w2_raw{half}", w2[:, half * H // 2 : (half + 1) * H // 2]) for half in range(2)]
         n2_sb = load_list("n2_sb", n2)
         gn_sb = load_rows("gn_sb", gn)
-        w2_raw = load_weight("w2_raw", w2)
         sl2_sb = load_rows("sl2_sb", sl2)
         th2_sb = load_rows("th2_sb", th2)
         w3_raw = load_weight("w3_raw", w3)
         n3_sb = load_list("n3_sb", n3)
         n4_sb = load_list("n4_sb", n4)
 
-        for q in range(4):
-            rows = slice(32 * q, 32 * q + 4)
-            nc.vector.tensor_copy(out=x_bytes[rows, :].bitcast(I32), in_=x_rows[rows, :].bitcast(I32))
+
+        w1_dealt = sb.tile([P, PACK * H], BF16, name="w1_dealt", align_bytes=64)
+        deal(nc.vector.tensor_copy, w1_dealt, w1_raw, 0, 64)
+        deal(nc.scalar.copy, w1_dealt, w1_raw, 64, P)
         picked_bytes = []
         for name, picks in (("y", offs_sb), ("d", two_sb)):
             got = sb.tile([P, S], U8, name=name + "_bytes", align_bytes=64)
             nc.vector.tensor_copy(got[:], x_bytes[:].indirect(picks[:]))
             picked_bytes.append(got)
-        bias1 = sb.tile([P, PACK], F32, name="bias1")
-        nc.vector.scalar_tensor_tensor(out=bias1[:], in0=sl_sb[:], scalar=-1.0, in1=th_sb[:], op0=ALU.mult, op1=ALU.mult)
 
-        w1_dealt = sb.tile([P, PACK * H], BF16, name="w1_dealt", align_bytes=64)
-        deal(nc.vector.tensor_copy, w1_dealt, w1_raw, 0, 64)
-        deal(nc.scalar.copy, w1_dealt, w1_raw, 64, P)
-        w1_q = [quantize(f"w1_{t}", w1_dealt[:, t * H : (t + 1) * H], P) for t in range(PACK)]
-        bias2 = sb.tile([P, PACK], F32, name="bias2")
-        nc.vector.scalar_tensor_tensor(out=bias2[:], in0=sl2_sb[:], scalar=-1.0, in1=th2_sb[:], op0=ALU.mult, op1=ALU.mult)
+        w1_q = quantize("w1", w1_dealt[:], H)
 
         picked = []
         for name, picks, got_bytes in (("y", offs_sb, picked_bytes[0]), ("d", two_sb, picked_bytes[1])):
             got = sb.tile([P, S], U32, name=name + "_words", align_bytes=64)
             nc.vector.tensor_copy(got[:], x_table[:].indirect(picks[:]))
-            picked.append((got, got_bytes))
+            picked.append((got[:], got_bytes[:]))
 
+        bias1 = neg_product("bias1", sl_sb, th_sb)
         y_ps, sg = [], []
         for t in range(PACK):
             acc = ps.tile([P, S], F32, name=f"y_ps{t}", tag=f"bank{t}")
-            product(acc[:], w1_q[t], picked[0])
+            product(acc[:], columns(w1_q, t), picked[0])
             y_ps.append(acc)
         for t in range(PACK):
-            y_sb = sb.tile([P, S], F32, name=f"y_sb{t}")
-            nc.vector.tensor_copy(out=y_sb[:], in_=y_ps[t][:])
+            y_sb = sb.tile([P, 2 * S], F32, name=f"y_sb{t}")
+            (nc.scalar.copy if t in (0, 1) else nc.vector.tensor_copy)(out=y_sb[:, 0:S], in_=y_ps[t][:])
             gate = sb.tile([P, S], F32, name=f"sg{t}")
-            for half in range(2):
-                nc.scalar.activation(
-                    out=gate[:, half * HALF : (half + 1) * HALF],
-                    in_=y_sb[:].indirect(half_list(n1_sb, half)),
-                    func=ACT.Sigmoid,
-                    bias=bias1[:, t : t + 1],
-                    scale=sl_sb[:, t : t + 1],
-                )
+            gather(gate[:], y_sb, n1_sb[:], ACT.Sigmoid, bias=bias1[:, t : t + 1], scale=sl_sb[:, t : t + 1])
             sg.append(gate)
 
         w2_dealt = sb.tile([P, PACK * H], BF16, name="w2_dealt", align_bytes=64)
-        deal(nc.vector.tensor_copy, w2_dealt, w2_raw, 0, P)
-        d_ps, d_sb = [], []
+        for half in range(2):
+            deal(nc.vector.tensor_copy, w2_dealt, w2_raw[half], half * P // 2, (half + 1) * P // 2, half * P // 2)
+        bias2 = neg_product("bias2", sl2_sb, th2_sb)
+        d_ps = []
         for t in range(PACK):
-            w2_q = quantize(f"w2_{t}", w2_dealt[:, t * H : (t + 1) * H], P)
+            if t % 2 == 0:
+                w2_q = quantize(f"w2_{t}", w2_dealt[:, t * H : (t + 2) * H], 2 * P)
             acc = ps.tile([P, S], F32, name=f"d_ps{t}", tag=f"bank{PACK + t}")
-            product(acc[:], w2_q, picked[1])
+            product(acc[:], columns(w2_q, t % 2), picked[1])
             d_ps.append(acc)
+        d_sb = [sb.tile([P, 2 * S], F32, name=f"d_sb{t}", tag=f"d_sb{t}", align_bytes=64) for t in range(PACK)]
         for t in range(PACK):
-            window = sb.tile([P, S], F32, name=f"d_sb{t}")
-            nc.scalar.copy(out=window[:], in_=d_ps[t][:])
-            d_sb.append(window)
+            (nc.scalar.copy if t in () else nc.vector.tensor_copy)(out=d_sb[t][:, 0:S], in_=d_ps[t][:])
+        sg2 = [sb.tile([P, S], F32, name=f"sg2_{t}") for t in range(PACK)]
+        for t in (0, 1):
+            gather(sg2[t][:], d_sb[t], n2_sb[:], ACT.Sigmoid, bias=bias2[:, t : t + 1], scale=sl2_sb[:, t : t + 1])
+        for half in range(2):
+            for t in (2, 3):
+                gather(sg2[t][:, half * HALF : (half + 1) * HALF], d_sb[t], half_list(n2_sb, half), ACT.Sigmoid,
+                       bias=bias2[:, t : t + 1], scale=sl2_sb[:, t : t + 1])
+
+        def deal_w3(copy, dealt, t):
+            copy(
+                out=dealt.rearrange("p (b c i j) -> p b c j i", c=2, i=4, j=PACK),
+                in_=w3_raw[:].rearrange("p j (b t c i) -> p t b c j i", t=PACK, c=2, i=4)[:, t],
+            )
+
         gated_d = sb.tile([P, PACK, S], F32, name="gated_d")
-        for t in range(PACK):
+        gated_y = sb.tile([P, 2, PACK, HALF], F32, name="gated_y")
+        z = [sb.tile([P, PACK * HALF], BF16, name=f"z{half}", tag=f"z{half}", align_bytes=64) for half in range(2)]
+        z_codes = sb.tile([P, S], U32, name="z_codes", align_bytes=64)
+        z_scales = sb.tile([P, S], U8, name="z_scales", align_bytes=64)
+
+        def gate_d(t):
             nc.vector.scalar_tensor_tensor(
                 out=gated_d[:, t, :], in0=sg[t][:], scalar=gn_sb[:, t : t + 1], in1=d_ps[t][:], op0=ALU.mult, op1=ALU.mult
             )
 
-        w3_dealt = sb.tile([P, PACK * H], BF16, name="w3_dealt", align_bytes=64)
-        deal(nc.vector.tensor_copy, w3_dealt, w3_raw, 0, P)
+        def gate_y(t, halves):
+            nc.vector.scalar_tensor_tensor(
+                out=gated_y[:, halves, t, :],
+                in0=sg2[t][:].rearrange("p (h c) -> p h c", h=2)[:, halves],
+                scalar=gn_sb[:, t : t + 1],
+                in1=y_ps[t][:].rearrange("p (h c) -> p h c", h=2)[:, halves],
+                op0=ALU.mult,
+                op1=ALU.mult,
+            )
 
-        w3_q = [quantize(f"w3_{t}", w3_dealt[:, t * H : (t + 1) * H], P) for t in range(PACK)]
-
-        sg2 = {}
-        for half in range(2):
-            for t in range(PACK):
-                gate = sb.tile([P, HALF], F32, name=f"sg2_{t}_{half}")
-                nc.scalar.activation(
-                    out=gate[:],
-                    in_=d_sb[t][:].indirect(half_list(n2_sb, half)),
-                    func=ACT.Sigmoid,
-                    bias=bias2[:, t : t + 1],
-                    scale=sl2_sb[:, t : t + 1],
-                )
-                sg2[t, half] = gate
-
-        z_q = []
-        for half in range(2):
-            cols = slice(half * HALF, (half + 1) * HALF)
-            gated_y = sb.tile([P, PACK, HALF], F32, name=f"gated_y{half}")
-            for t in range(PACK):
-                nc.vector.scalar_tensor_tensor(
-                    out=gated_y[:, t, :], in0=sg2[t, half][:], scalar=gn_sb[:, t : t + 1], in1=y_ps[t][:, cols],
-                    op0=ALU.mult, op1=ALU.mult,
-                )
-            z = sb.tile([P, PACK * HALF], BF16, name=f"z{half}", align_bytes=64)
+        def add_z(half):
             nc.vector.tensor_tensor(
-                out=z[:].rearrange("p (c i t) -> p c t i", i=4, t=PACK),
-                in0=gated_d[:, :, cols].rearrange("p t (c i) -> p c t i", i=4),
-                in1=gated_y[:].rearrange("p t (c i) -> p c t i", i=4),
+                out=z[half][:].rearrange("p (c i t) -> p c t i", i=4, t=PACK),
+                in0=gated_d[:, :, half * HALF : (half + 1) * HALF].rearrange("p t (c i) -> p c t i", i=4),
+                in1=gated_y[:, half].rearrange("p t (c i) -> p c t i", i=4),
                 op=ALU.add,
             )
-            z_q.append(quantize(f"z{half}", z[:], HALF))
 
-        h_sb = [sb.tile([P, S], F32, name=f"h_sb{t}") for t in range(PACK)]
+        def quantize_z(half):
+            cols = slice(half * HALF, (half + 1) * HALF)
+            nc.vector.quantize_mx(out=z_codes[:, cols].bitcast(FP8X4), scales=z_scales[:, cols], in_=z[half][:])
+
+        both = slice(0, 2)
+        w3_first = sb.tile([P, H], BF16, name="w3_first", align_bytes=64)
+        deal_w3(nc.vector.tensor_copy, w3_first[:], 0)
+        gate_d(0)
+        gate_d(1)
+        gate_y(0, both)
+        w3_q = [quantize("w3_0", w3_first[:], P)]
+        gate_d(2)
+        gate_d(3)
+        gate_y(1, both)
+        gate_y(2, slice(0, 1))
+        gate_y(3, slice(0, 1))
+        add_z(0)
+        gate_y(2, slice(1, 2))
+        quantize_z(0)
+        gate_y(3, slice(1, 2))
+        add_z(1)
+        quantize_z(1)
+        w3_late = sb.tile([P, (PACK - 1) * H], BF16, name="w3_late", tag=f"d_sb{PACK - 1}", align_bytes=64)
+        for t in range(1, PACK):
+            deal_w3(nc.scalar.copy, w3_late[:, (t - 1) * H : t * H], t)
+
+        h_sb = [sb.tile([P, 2 * S], F32, name=f"h_sb{t}") for t in range(PACK)]
         for half in range(2):
-            for t in range(PACK):
-                acc = ps.tile([P, HALF], F32, name=f"h_ps{t}_{half}", tag=f"bank{PACK * (1 - half) + t}")
-                product(acc[:], w3_q[t], z_q[half])
-                nc.vector.tensor_copy(out=h_sb[t][:, half * HALF : (half + 1) * HALF], in_=acc[:])
+            cols = slice(half * HALF, (half + 1) * HALF)
+            acc = ps.tile([P, HALF], F32, name=f"h_ps0_{half}", tag=f"bank{PACK * (1 - half)}")
+            product(acc[:], w3_q[0], (z_codes[:, cols], z_scales[:, cols]))
+            nc.scalar.copy(out=h_sb[0][:, cols], in_=acc[:])
+        w3_rest = quantize("w3_late", w3_late[:], (PACK - 1) * P, tag="z1")
+        for t in range(1, PACK):
+            acc = ps.tile([P, S], F32, name=f"h_ps{t}", tag=f"bank{PACK + t}")
+            product(acc[:], columns(w3_rest, t - 1), (z_codes[:], z_scales[:]))
+            nc.vector.tensor_copy(out=h_sb[t][:, 0:S], in_=acc[:])
 
-        out_rows = out.rearrange("(p t) j -> p t j", t=PACK)
+        out_rows = out.rearrange("(b t q) j -> t b q j", t=PACK, q=8)
         for t in range(PACK):
             at_n3 = sb.tile([P, S], F32, name=f"at_n3_{t}")
             at_n4 = sb.tile([P, S], F32, name=f"at_n4_{t}")
-            for half in range(2):
-                nc.scalar.activation(
-                    out=at_n3[:, half * HALF : (half + 1) * HALF], in_=h_sb[t][:].indirect(half_list(n3_sb, half)), func=ACT.Copy
-                )
-            for half in range(2):
-                nc.scalar.activation(
-                    out=at_n4[:, half * HALF : (half + 1) * HALF], in_=h_sb[t][:].indirect(half_list(n4_sb, half)),
-                    func=ACT.Copy, scale=0.5,
-                )
+            gather(at_n3[:], h_sb[t], n3_sb[:], ACT.Copy)
             above = sb.tile([P, S], F32, name=f"above{t}")
-            nc.vector.tensor_tensor(out=above[:], in0=h_sb[t][:], in1=at_n3[:], op=ALU.subtract)
+            nc.vector.tensor_tensor(out=above[:], in0=h_sb[t][:, 0:S], in1=at_n3[:], op=ALU.subtract)
             hinge = sb.tile([P, S], F32, name=f"hinge{t}")
-            nc.vector.tensor_scalar(out=hinge[:], in0=above[:], scalar1=0.0, scalar2=None, op0=ALU.max)
+            nc.vector.tensor_scalar(out=hinge[:], in0=above[:], scalar1=0.0, scalar2=0.0, op0=ALU.max, op1=ALU.add)
             below = sb.tile([P, S], F32, name=f"below{t}")
             result = sb.tile([P, S], F32, name=f"result{t}")
-            pieces = [slice(0, HALF), slice(HALF, S)] if t == PACK - 1 else [slice(0, S)]
-            for cols in pieces:
+            pieces = [0, 1] if t == PACK - 1 else [None]
+            for half in pieces:
+                cols = slice(0, S) if half is None else slice(half * HALF, (half + 1) * HALF)
+                gather(at_n4[:, cols], h_sb[t], n4_sb[:] if half is None else half_list(n4_sb, half), ACT.Copy, scale=0.5)
                 nc.vector.scalar_tensor_tensor(
                     out=below[:, cols], in0=h_sb[t][:, cols], scalar=-0.5, in1=at_n4[:, cols], op0=ALU.mult, op1=ALU.add
                 )
                 nc.vector.scalar_tensor_tensor(
                     out=result[:, cols], in0=below[:, cols], scalar=0.0, in1=hinge[:, cols], op0=ALU.max, op1=ALU.add
                 )
-                nc.sync.dma_start(out=out_rows[:, t, cols], in_=result[:, cols])
+                nc.sync.dma_start(out=out_rows[t][:, :, cols], in_=result[:, cols])

from contextlib import ExitStack

import concourse.mybir as mybir

K, T, S, H, N = 512, 2048, 256, 512, 512
FLOPS = 2 * K * H * S * 2 + 2 * H * N * S

F32 = mybir.dt.float32
BF16 = mybir.dt.bfloat16
I32 = mybir.dt.int32
U32 = mybir.dt.uint32
U16 = mybir.dt.uint16
U8 = mybir.dt.uint8
FP8X4 = mybir.dt.float8_e4m3fn_x4
ALU = mybir.AluOpType
ACT = mybir.ActivationFunctionType

P = 128
PACK = 4
HALF = S // 2
LIST_COLS = S // 16


def tile_picked_twlcxbhinge_none_p_kernel(
    tc, x_words, x_scales, w1, w2, sl, th, sl2, th2, gn, w3, offs, two, n1, n2, n3, n4, out
):
    nc = tc.nc
    with ExitStack() as ctx:
        sb = ctx.enter_context(tc.tile_pool(name="sb", bufs=1))
        ps = ctx.enter_context(tc.psum_pool(name="ps", bufs=1))

        def load_list(name, src):
            tile = sb.tile([P, LIST_COLS], U16, name=name)
            nc.sync.dma_start(tile[:], src)
            return tile

        def load_weight(name, src):
            tile = sb.tile([P, PACK, src.shape[1]], F32, name=name)
            nc.sync.dma_start(out=tile[:], in_=src.rearrange("(p j) c -> p j c", j=PACK))
            return tile

        def load_rows(name, src):
            tile = sb.tile([P, PACK], F32, name=name)
            nc.sync.dma_start(out=tile[:], in_=src.rearrange("(p t) o -> p (t o)", t=PACK))
            return tile

        def half_list(tile, half):
            return tile[:, half * LIST_COLS // 2 : (half + 1) * LIST_COLS // 2]

        def deal(copy, dealt, raw, m0, m1, first=0):
            copy(
                out=dealt[:].rearrange("p (t m j) -> p m j t", t=PACK, j=PACK)[:, m0:m1],
                in_=raw[:].rearrange("p j (m t) -> p m j t", t=PACK)[:, m0 - first : m1 - first],
            )

        def quantize(name, values, width, tag=None):
            codes = sb.tile([P, width], U32, name=name + "_codes", tag=tag or name + "_codes", align_bytes=64)
            scales = sb.tile([P, width], U8, name=name + "_scales", align_bytes=64)
            nc.vector.quantize_mx(out=codes[:].bitcast(FP8X4), scales=scales[:], in_=values)
            return codes[:], scales[:]

        def columns(operand, t):
            return operand[0][:, t * P : (t + 1) * P], operand[1][:, t * P : (t + 1) * P]

        def product(acc, lhs, rhs):
            nc.tensor.matmul_mx(
                out=acc,
                lhsT=lhs[0].bitcast(FP8X4),
                lhsT_scale=lhs[1],
                rhs=rhs[0].bitcast(FP8X4),
                rhs_scale=rhs[1],
                start=True,
                stop=True,
            )

        def gather(out_ap, window, picks, func, **kw):
            nc.scalar.activation(out=out_ap, in_=window[:].indirect(picks), func=func, **kw)

        def neg_product(name, a, b):
            prod = sb.tile([P, PACK], F32, name=name + "_prod")
            nc.gpsimd.tensor_tensor(out=prod[:], in0=a[:], in1=b[:], op=ALU.mult)
            neg = sb.tile([P, PACK], F32, name=name)
            nc.gpsimd.tensor_scalar(out=neg[:], in0=prod[:], scalar1=-1.0, scalar2=0.0, op0=ALU.mult, op1=ALU.add)
            return neg

        x_bytes = sb.tile([P, T], U8, name="x_bytes", align_bytes=64)
        nc.vector.memset(x_bytes[:].bitcast(I32), 0)
        w1_raw = load_weight("w1_raw", w1)
        for q in range(4):
            nc.sync.dma_start(out=x_bytes[32 * q : 32 * q + 4, :].bitcast(I32), in_=x_scales[0][4 * q : 4 * q + 4, :].bitcast(I32))
        offs_sb = load_list("offs_sb", offs)
        two_sb = load_list("two_sb", two)
        x_table = sb.tile([P, T], U32, name="x_table", align_bytes=64)
        nc.sync.dma_start(out=x_table[:].bitcast(I32), in_=x_words[0].rearrange("p c r -> p (c r)").bitcast(I32))
        sl_sb = load_rows("sl_sb", sl)
        th_sb = load_rows("th_sb", th)
        n1_sb = load_list("n1_sb", n1)
        w2_raw = [load_weight(f"w2_raw{half}", w2[:, half * H // 2 : (half + 1) * H // 2]) for half in range(2)]
        n2_sb = load_list("n2_sb", n2)
        gn_sb = load_rows("gn_sb", gn)
        sl2_sb = load_rows("sl2_sb", sl2)
        th2_sb = load_rows("th2_sb", th2)
        w3_raw = load_weight("w3_raw", w3)
        n3_sb = load_list("n3_sb", n3)
        n4_sb = load_list("n4_sb", n4)


        w1_dealt = sb.tile([P, PACK * H], BF16, name="w1_dealt", align_bytes=64)
        deal(nc.vector.tensor_copy, w1_dealt, w1_raw, 0, 64)
        deal(nc.scalar.copy, w1_dealt, w1_raw, 64, P)
        picked_bytes = []
        for name, picks in (("y", offs_sb), ("d", two_sb)):
            got = sb.tile([P, S], U8, name=name + "_bytes", align_bytes=64)
            nc.vector.tensor_copy(got[:], x_bytes[:].indirect(picks[:]))
            picked_bytes.append(got)

        w1_q = quantize("w1", w1_dealt[:], H)

        picked = []
        for name, picks, got_bytes in (("y", offs_sb, picked_bytes[0]), ("d", two_sb, picked_bytes[1])):
            got = sb.tile([P, S], U32, name=name + "_words", align_bytes=64)
            nc.vector.tensor_copy(got[:], x_table[:].indirect(picks[:]))
            picked.append((got[:], got_bytes[:]))

        bias1 = neg_product("bias1", sl_sb, th_sb)
        y_ps, sg = [], []
        for t in range(PACK):
            acc = ps.tile([P, S], F32, name=f"y_ps{t}", tag=f"bank{t}")
            product(acc[:], columns(w1_q, t), picked[0])
            y_ps.append(acc)
        for t in range(PACK):
            y_sb = sb.tile([P, 2 * S], F32, name=f"y_sb{t}")
            (nc.scalar.copy if t in (0, 1) else nc.vector.tensor_copy)(out=y_sb[:, 0:S], in_=y_ps[t][:])
            gate = sb.tile([P, S], F32, name=f"sg{t}")
            gather(gate[:], y_sb, n1_sb[:], ACT.Sigmoid, bias=bias1[:, t : t + 1], scale=sl_sb[:, t : t + 1])
            sg.append(gate)

        w2_dealt = sb.tile([P, PACK * H], BF16, name="w2_dealt", align_bytes=64)
        for half in range(2):
            deal(nc.vector.tensor_copy, w2_dealt, w2_raw[half], half * P // 2, (half + 1) * P // 2, half * P // 2)
        bias2 = neg_product("bias2", sl2_sb, th2_sb)
        d_ps = []
        for t in range(PACK):
            if t % 2 == 0:
                w2_q = quantize(f"w2_{t}", w2_dealt[:, t * H : (t + 2) * H], 2 * P)
            acc = ps.tile([P, S], F32, name=f"d_ps{t}", tag=f"bank{PACK + t}")
            product(acc[:], columns(w2_q, t % 2), picked[1])
            d_ps.append(acc)
        d_sb = [sb.tile([P, 2 * S], F32, name=f"d_sb{t}", tag=f"d_sb{t}", align_bytes=64) for t in range(PACK)]
        for t in range(PACK):
            (nc.scalar.copy if t in () else nc.vector.tensor_copy)(out=d_sb[t][:, 0:S], in_=d_ps[t][:])
        sg2 = [sb.tile([P, S], F32, name=f"sg2_{t}") for t in range(PACK)]
        for t in (0, 1):
            gather(sg2[t][:], d_sb[t], n2_sb[:], ACT.Sigmoid, bias=bias2[:, t : t + 1], scale=sl2_sb[:, t : t + 1])
        for half in range(2):
            for t in (2, 3):
                gather(sg2[t][:, half * HALF : (half + 1) * HALF], d_sb[t], half_list(n2_sb, half), ACT.Sigmoid,
                       bias=bias2[:, t : t + 1], scale=sl2_sb[:, t : t + 1])

        def deal_w3(copy, dealt, t):
            copy(
                out=dealt.rearrange("p (b c i j) -> p b c j i", c=2, i=4, j=PACK),
                in_=w3_raw[:].rearrange("p j (b t c i) -> p t b c j i", t=PACK, c=2, i=4)[:, t],
            )

        gated_d = sb.tile([P, PACK, S], F32, name="gated_d")
        gated_y = sb.tile([P, 2, PACK, HALF], F32, name="gated_y")
        z = [sb.tile([P, PACK * HALF], BF16, name=f"z{half}", tag=f"z{half}", align_bytes=64) for half in range(2)]
        z_codes = sb.tile([P, S], U32, name="z_codes", align_bytes=64)
        z_scales = sb.tile([P, S], U8, name="z_scales", align_bytes=64)

        def gate_d(t):
            nc.vector.scalar_tensor_tensor(
                out=gated_d[:, t, :], in0=sg[t][:], scalar=gn_sb[:, t : t + 1], in1=d_ps[t][:], op0=ALU.mult, op1=ALU.mult
            )

        def gate_y(t, halves):
            nc.vector.scalar_tensor_tensor(
                out=gated_y[:, halves, t, :],
                in0=sg2[t][:].rearrange("p (h c) -> p h c", h=2)[:, halves],
                scalar=gn_sb[:, t : t + 1],
                in1=y_ps[t][:].rearrange("p (h c) -> p h c", h=2)[:, halves],
                op0=ALU.mult,
                op1=ALU.mult,
            )

        def add_z(half):
            nc.vector.tensor_tensor(
                out=z[half][:].rearrange("p (c i t) -> p c t i", i=4, t=PACK),
                in0=gated_d[:, :, half * HALF : (half + 1) * HALF].rearrange("p t (c i) -> p c t i", i=4),
                in1=gated_y[:, half].rearrange("p t (c i) -> p c t i", i=4),
                op=ALU.add,
            )

        def quantize_z(half):
            cols = slice(half * HALF, (half + 1) * HALF)
            nc.vector.quantize_mx(out=z_codes[:, cols].bitcast(FP8X4), scales=z_scales[:, cols], in_=z[half][:])

        both = slice(0, 2)
        w3_first = sb.tile([P, H], BF16, name="w3_first", align_bytes=64)
        deal_w3(nc.vector.tensor_copy, w3_first[:], 0)
        gate_d(0)
        gate_d(1)
        gate_y(0, both)
        w3_q = [quantize("w3_0", w3_first[:], P)]
        gate_d(2)
        gate_d(3)
        gate_y(1, both)
        gate_y(2, slice(0, 1))
        gate_y(3, slice(0, 1))
        add_z(0)
        gate_y(2, slice(1, 2))
        quantize_z(0)
        gate_y(3, slice(1, 2))
        add_z(1)
        quantize_z(1)
        w3_late = sb.tile([P, (PACK - 1) * H], BF16, name="w3_late", tag=f"d_sb{PACK - 1}", align_bytes=64)
        for t in range(1, PACK):
            deal_w3(nc.scalar.copy, w3_late[:, (t - 1) * H : t * H], t)

        h_sb = [sb.tile([P, 2 * S], F32, name=f"h_sb{t}") for t in range(PACK)]
        for half in range(2):
            cols = slice(half * HALF, (half + 1) * HALF)
            acc = ps.tile([P, HALF], F32, name=f"h_ps0_{half}", tag=f"bank{PACK * (1 - half)}")
            product(acc[:], w3_q[0], (z_codes[:, cols], z_scales[:, cols]))
            nc.scalar.copy(out=h_sb[0][:, cols], in_=acc[:])
        w3_rest = quantize("w3_late", w3_late[:], (PACK - 1) * P, tag="z1")
        for t in range(1, PACK):
            acc = ps.tile([P, S], F32, name=f"h_ps{t}", tag=f"bank{PACK + t}")
            product(acc[:], columns(w3_rest, t - 1), (z_codes[:], z_scales[:]))
            nc.vector.tensor_copy(out=h_sb[t][:, 0:S], in_=acc[:])

        out_rows = out.rearrange("(b t q) j -> t b q j", t=PACK, q=8)
        for t in range(PACK):
            at_n3 = sb.tile([P, S], F32, name=f"at_n3_{t}")
            at_n4 = sb.tile([P, S], F32, name=f"at_n4_{t}")
            gather(at_n3[:], h_sb[t], n3_sb[:], ACT.Copy)
            above = sb.tile([P, S], F32, name=f"above{t}")
            nc.vector.tensor_tensor(out=above[:], in0=h_sb[t][:, 0:S], in1=at_n3[:], op=ALU.subtract)
            hinge = sb.tile([P, S], F32, name=f"hinge{t}")
            nc.vector.tensor_scalar(out=hinge[:], in0=above[:], scalar1=0.0, scalar2=0.0, op0=ALU.max, op1=ALU.add)
            below = sb.tile([P, S], F32, name=f"below{t}")
            result = sb.tile([P, S], F32, name=f"result{t}")
            pieces = [0, 1] if t == PACK - 1 else [None]
            for half in pieces:
                cols = slice(0, S) if half is None else slice(half * HALF, (half + 1) * HALF)
                gather(at_n4[:, cols], h_sb[t], n4_sb[:] if half is None else half_list(n4_sb, half), ACT.Copy, scale=0.5)
                nc.vector.scalar_tensor_tensor(
                    out=below[:, cols], in0=h_sb[t][:, cols], scalar=-0.5, in1=at_n4[:, cols], op0=ALU.mult, op1=ALU.add
                )
                nc.vector.scalar_tensor_tensor(
                    out=result[:, cols], in0=below[:, cols], scalar=0.0, in1=hinge[:, cols], op0=ALU.max, op1=ALU.add
                )
                nc.sync.dma_start(out=out_rows[t][:, :, cols], in_=result[:, cols])
